import numpy as np
import ml_dtypes


def mxq(x, axis, fmt="e4m3"):
    dtype, down = {"e4m3": (ml_dtypes.float8_e4m3fn, 7), "e5m2": (ml_dtypes.float8_e5m2, 14)}[fmt]
    v = np.moveaxis(np.asarray(x, np.float32).astype(ml_dtypes.bfloat16).astype(np.float64), axis, -1)
    blocks = v.reshape(v.shape[:-1] + (-1, 32))
    amax = np.abs(blocks).max(-1, keepdims=True)
    byte = np.maximum(np.where(amax > 0, np.frexp(amax)[1] - 1 + 127, 0) - down, 1)
    scale = np.exp2(byte - 127.0)
    codes = (blocks / scale).astype(np.float32).astype(dtype).astype(np.float64)
    return np.moveaxis((codes * scale).reshape(v.shape), -1, axis)


WIDE = False


def mx_kscale(k):
    if not WIDE:
        return np.ones(k)
    levels = np.array([10, -10, 5, -5, 0])
    if k % 512:
        return np.exp2(np.random.permutation(np.resize(levels, k // 32))).repeat(32)
    a = np.empty((k // 512, 16))
    for p in range(k // 512):
        a[p, :8] = np.random.permutation(np.resize(levels, 8))
        for g in range(8):
            far = levels[np.abs(levels - a[p, g]) >= 10]
            a[p, g + 8] = far[np.random.randint(len(far))]
    return np.exp2(a.ravel()).repeat(32)


def f64(x):
    return np.asarray(x).astype(np.float64)


def striped(idx):
    return np.tile(np.asarray(idx).reshape(-1, 16).T, (8, 1)).astype(np.uint16)


def unstriped(offs):
    return offs[:16].T.reshape(-1).astype(np.int64)


E2M1 = np.array([0.0, 0.5, 1.0, 1.5, 2.0, 3.0, 4.0, 6.0, -0.0, -0.5, -1.0, -1.5, -2.0, -3.0, -4.0, -6.0])


def pack_weight(w, fmt):
    k, n = w.shape
    w = f64(np.asarray(w, np.float32).astype(ml_dtypes.bfloat16)).reshape(k // 32, 32, n)
    amax = np.abs(w).max(1)
    if fmt == "e4m3":
        byte = np.frexp(amax)[1] - 1 + 127 - 7
    else:
        mant, ex = np.frexp(amax / 6.0)
        byte = np.where(mant > 0.5, ex, ex - 1) + 127
    byte = np.clip(np.where(amax > 0, byte, 1), 1, 254)
    scaled = (w * np.exp2(127.0 - byte)[:, None, :]).reshape(k, n).astype(np.float32)
    by_word = np.ascontiguousarray(scaled.reshape(k // 512, 128, 4, n).transpose(0, 1, 3, 2))
    if fmt == "e4m3":
        words = by_word.astype(ml_dtypes.float8_e4m3fn).view(np.uint8)
    else:
        c = by_word.astype(ml_dtypes.float4_e2m1fn).view(np.uint8) & 0xF
        words = (c[..., 0::2] | (c[..., 1::2] << 4)).reshape(k // 512, 128, 2 * n)
    return np.ascontiguousarray(words), np.ascontiguousarray(byte.astype(np.uint8).reshape(k // 512, 16, n))


def unpack_weight(words, scales, fmt):
    g, _, n = scales.shape
    words = np.ascontiguousarray(words).reshape(g, 128, n, -1)
    if fmt == "e4m3":
        vals = words.view(ml_dtypes.float8_e4m3fn).astype(np.float64)
    else:
        nib = np.empty((g, 128, n, 4), np.uint8)
        nib[..., 0::2] = words & 0xF
        nib[..., 1::2] = words >> 4
        vals = E2M1[nib]
    vals = vals * np.repeat(np.exp2(scales.astype(np.float64) - 127.0), 8, axis=1)[..., None]
    return vals.transpose(0, 1, 3, 2).reshape(g * 512, n)


def bf(x):
    return np.asarray(x, np.float32).astype(ml_dtypes.bfloat16)


def planes(Y):
    r, m = Y.shape
    b = f64(bf(Y)).reshape(r // 32, 32, m)
    amax = np.abs(b).max(1)
    byte = np.clip(np.where(amax > 0, np.frexp(amax)[1] - 1 + 127 - 7, 1), 1, 254)
    codes = (b * np.exp2(127.0 - byte)[:, None, :]).reshape(r, m).astype(np.float32).astype(ml_dtypes.float8_e4m3fn).view(np.uint8)
    words = codes.reshape(r // 512, 128, 4, m).transpose(0, 1, 3, 2)
    return np.ascontiguousarray(words), np.ascontiguousarray(byte.astype(np.uint8).reshape(r // 512, 16, m))


K, T, J, N = 1024, 2048, 512, 512


def setup_inputs():
    n = np.random.standard_normal
    idx = np.random.permutation(T)[:J]
    idx2 = np.random.permutation(T)[:J]
    fk = mx_kscale(K)
    wap = pack_weight(n((K, N)) * 1 / np.sqrt(K) * fk[:, None], "e2m1")
    wbp = pack_weight(n((K, N)) * 1 / np.sqrt(K) * fk[:, None], "e4m3")
    return {
        "xt": (n((K, T)) * np.random.uniform(0.3, 1.7, (1, T)) / fk[:, None]).astype(np.float32),
        "wa_words": wap[0],
        "wa_scales": wap[1],
        "wb_words": wbp[0],
        "wb_scales": wbp[1],
        "of": (np.random.uniform(0.0, 1.5, (1, N))).astype(np.float32),
        "offs": striped(idx),
        "offs2": striped(idx2),
    }


def reference(xt, wa_words, wa_scales, wb_words, wb_scales, of, offs, offs2):
    idx = unstriped(offs)
    idx2 = unstriped(offs2)
    wau = unpack_weight(wa_words, wa_scales, "e2m1")
    wbu = unpack_weight(wb_words, wb_scales, "e4m3")
    xtidxq = mxq(f64(xt)[:, idx], 0, "e4m3")
    a = xtidxq.T @ wau
    xtidx2q = mxq(f64(xt)[:, idx2], 0, "e4m3")
    b = xtidx2q.T @ wbu
    m = np.max(b, axis=1, keepdims=True)
    y = np.maximum(a + f64(of) - m + 3.0, 0.0)
    words, scales = planes(y)
    return y, words, scales

@@ -1,0 +1,211 @@
+from contextlib import ExitStack
+
+import concourse.mybir as mybir
+from concourse.masks import make_identity
+
+K, T, J, N = 1024, 2048, 512, 512
+FLOPS = 2 * 2 * K * J * N
+
+F32 = mybir.dt.float32
+BF16 = mybir.dt.bfloat16
+I32 = mybir.dt.int32
+U32 = mybir.dt.uint32
+U16 = mybir.dt.uint16
+U8 = mybir.dt.uint8
+FP8X4 = mybir.dt.float8_e4m3fn_x4
+FP4X4 = mybir.dt.float4_e2m1fn_x4
+ALU = mybir.AluOpType
+ACT = mybir.ActivationFunctionType
+
+P = 128
+PASSES = 2
+CHUNKS = [
+    [(0, 1024, 1024), (1024, 1024, 384)],
+    [(0, 1024, 1024), (1024, 1024, 384)],
+    [(0, 512, 512), (512, 512, 512), (1024, 512, 512), (1536, 512, 512)],
+    [(0, 512, 512), (512, 512, 512), (1024, 512, 352), (1536, 256, 0), (1792, 256, 64)],
+]
+ROUND_ON_SCALAR = 192
+
+
+def tile_moe_expert_rows_against_best_of_other_pl_kernel(
+    tc, xt, wa_words, wa_scales, wb_words, wb_scales, of, offs, offs2, out_0, out_1, out_2
+):
+    nc = tc.nc
+    with ExitStack() as ctx:
+        keep = ctx.enter_context(tc.tile_pool(name="keep", bufs=1))
+        psum = ctx.enter_context(tc.psum_pool(name="psum", bufs=1))
+
+        list_a = keep.tile([P, J // 16], U16, name="list_a")
+        list_b = keep.tile([P, J // 16], U16, name="list_b")
+        lists = {"a": list_a, "b": list_b}
+        w_scales = keep.tile([P, 2, PASSES, N], U8, name="w_scales", align_bytes=64)
+        of_cols = keep.tile([P, 4], F32, name="of_cols")
+        ident = keep.tile([P, P], F32, name="ident")
+        of3 = keep.tile([P, N], F32, name="of3")
+        banks = {e: [psum.tile([P, N], F32, name=f"ps_{e}{t}") for t in range(4)] for e in "ba"}
+
+        nc.vector.memset(w_scales[:].rearrange("p w g n -> p (w g n)").bitcast(I32), 0)
+        make_identity(nc, ident[:])
+
+        x_rows = xt.rearrange("(g p u e) c -> g u p e c", g=PASSES, p=P, u=2, e=2)
+        pairs = [(g, u) for g in range(PASSES) for u in range(2)]
+        raw = {}
+
+        def load_x(i, c):
+            g, u = pairs[i]
+            c0, width, s_cols = CHUNKS[i][c]
+            raw[i, c] = keep.tile([P, 2, width], F32, name=f"raw{i}_{c}")
+            nc.sync.dma_start(out=raw[i, c][:], in_=x_rows[g, u][:, :, c0 : c0 + width])
+
+        def load_scales(w, r):
+            src = (wb_scales, wa_scales)[w]
+            nc.sync.dma_start(
+                out=w_scales[r:P:32, w].bitcast(I32),
+                in_=src.rearrange("g (q r) n -> r q g n", r=4)[r].bitcast(I32),
+            )
+
+        load_x(0, 0)
+        load_x(0, 1)
+        nc.sync.dma_start(list_b[:], offs2)
+        nc.sync.dma_start(list_a[:], offs)
+        nc.sync.dma_start(out=of_cols[:], in_=of.rearrange("o (p c) -> (o p) c", c=4))
+        for r in range(3):
+            load_scales(0, r)
+        load_x(1, 0)
+        load_scales(0, 3)
+        load_x(1, 1)
+        for r in range(4):
+            load_scales(1, r)
+        for i in (2, 3):
+            for c in range(len(CHUNKS[i])):
+                load_x(i, c)
+        w_words = {}
+        for g in range(PASSES):
+            wb = keep.tile([P, N], I32, name=f"wb{g}", align_bytes=64)
+            nc.sync.dma_start(out=wb[:], in_=wb_words[g].rearrange("p n t -> p (n t)").bitcast(I32))
+            w_words["b", g] = wb[:].bitcast(FP8X4)
+        wa = keep.tile([P, PASSES, 2 * N], U8, name="wa", align_bytes=64)
+        nc.sync.dma_start(out=wa[:].bitcast(I32), in_=wa_words.rearrange("g p c -> p g c").bitcast(I32))
+        for g in range(PASSES):
+            w_words["a", g] = wa[:, g, :].bitcast(FP4X4)
+
+        spread = banks["a"][3]
+        for c in range(4):
+            nc.tensor.transpose(spread[:, c * P : (c + 1) * P], of_cols[:, c : c + 1].to_broadcast([P, P]), ident[:])
+        nc.vector.tensor_scalar_add(
+            of3[:].rearrange("q (p c) -> q p c", c=4), spread[:].rearrange("q (c p) -> q p c", c=4), 3.0
+        )
+
+        picked = {(e, g): keep.tile([P, 2, J], U32, name=f"picked_{e}{g}") for e in "ba" for g in range(PASSES)}
+        codes, scales = {}, {}
+
+        def cast_pair(i):
+            window = keep.tile([P, T, 2], BF16, name=f"window{i}")
+            for c, (c0, width, s_cols) in enumerate(CHUNKS[i]):
+                src = raw[i, c][:].rearrange("p e c -> p c e")
+                if s_cols > 0:
+                    nc.scalar.activation(window[:, c0 : c0 + s_cols, :], src[:, 0:s_cols, :], ACT.Copy)
+                if s_cols < width:
+                    nc.vector.tensor_copy(window[:, c0 + s_cols : c0 + width, :], src[:, s_cols:width, :])
+            return window
+
+        def gather(i, window, e, j0, j1):
+            g, u = pairs[i]
+            words = window[:].rearrange("p c e -> p (c e)").bitcast(U32)
+            nc.vector.tensor_copy(picked[e, g][:, u, j0:j1], words.indirect(lists[e][:, j0 // 16 : j1 // 16]))
+
+        woven = {
+            (e, g): keep.tile([P, 4 * J], BF16, name=f"woven_{e}{g}", align_bytes=64)
+            for e in "ba"
+            for g in range(PASSES)
+        }
+
+        def weave(e, g, j0, j1, on_scalar):
+            word = U32 if on_scalar else I32
+            dst = woven[e, g][:].bitcast(word).rearrange("q (t p u) -> q p t u", t=4, u=2)[:, j0 // 4 : j1 // 4]
+            src = picked[e, g][:, :, j0:j1].bitcast(word).rearrange("q u (p t) -> q p t u", t=4)
+            if on_scalar:
+                nc.scalar.copy(dst, src)
+            else:
+                nc.vector.tensor_copy(dst, src)
+
+        def quantise(e, g):
+            codes[e, g] = keep.tile([P, J], U32, name=f"codes_{e}{g}", align_bytes=64)
+            scales[e, g] = keep.tile([P, J], U8, name=f"scales_{e}{g}", align_bytes=64)
+            nc.vector.quantize_mx(out=codes[e, g][:].bitcast(FP8X4), scales=scales[e, g][:], in_=woven[e, g][:])
+
+        def multiply(e, g, t):
+            if True:
+                cols = slice(t * P, (t + 1) * P)
+                nc.tensor.matmul_mx(
+                    out=banks[e][t][:],
+                    lhsT=codes[e, g][:, cols].bitcast(FP8X4),
+                    lhsT_scale=scales[e, g][:, cols],
+                    rhs=w_words[e, g],
+                    rhs_scale=w_scales[:, "ba".index(e), g, :],
+                    start=(g == 0),
+                    stop=(g == PASSES - 1),
+                )
+
+        for i in range(3):
+            window = cast_pair(i)
+            for e in "ba":
+                gather(i, window, e, 0, J)
+            if i == 1:
+                for e in "ba":
+                    weave(e, 0, 0, J, False)
+                for e in "ba":
+                    quantise(e, 0)
+        window = cast_pair(3)
+        for e in "ba":
+            for j0 in (0, J // 2):
+                gather(3, window, e, j0, j0 + J // 2)
+                weave(e, 1, j0, j0 + J // 2, True)
+        for e in "ba":
+            quantise(e, 1)
+        for g in range(PASSES):
+            for t in range(4):
+                multiply("b", g, t)
+        for t in range(4):
+            for g in range(PASSES):
+                multiply("a", g, t)
+
+        best = keep.tile([P, 4], F32, name="best")
+        for t in range(4):
+            nc.vector.tensor_reduce(best[:, t : t + 1], banks["b"][t][:], mybir.AxisListType.X, ALU.max)
+        excess = keep.tile([P, 4, N], F32, name="excess")
+        out_rows = out_0.rearrange("(p t) n -> p t n", t=4)
+        half = N // 2
+        rounded = [keep.tile([P, half, 4], BF16, name=f"rounded{h}", align_bytes=64) for h in range(2)]
+        by_column = excess[:].rearrange("p t n -> p n t")
+        split = half - ROUND_ON_SCALAR
+        for t in range(4):
+            nc.vector.scalar_tensor_tensor(
+                excess[:, t, :], banks["a"][t][:], best[:, t : t + 1], of3[:], ALU.subtract, ALU.add
+            )
+            if t == 3:
+                nc.scalar.activation(rounded[1][:, split:half, :], by_column[:, half + split : N, :], ACT.Relu)
+            y = keep.tile([P, N], F32, name=f"y{t}")
+            nc.scalar.activation(y[:], excess[:, t, :], ACT.Relu)
+            nc.sync.dma_start(out=out_rows[:, t, :], in_=y[:])
+
+        y_codes = keep.tile([P, N], U32, name="y_codes", align_bytes=64)
+        y_scales = keep.tile([P, N], U8, name="y_scales", align_bytes=64)
+        nc.vector.tensor_scalar_max(rounded[0][:], by_column[:, 0:half, :], 0.0)
+        nc.vector.tensor_scalar_max(rounded[1][:, 0:split, :], by_column[:, half : half + split, :], 0.0)
+        words_out = out_1[0].rearrange("p n t -> p (n t)").bitcast(I32)
+        for h in range(2):
+            cols = slice(h * half, (h + 1) * half)
+            nc.vector.quantize_mx(
+                out=y_codes[:, cols].bitcast(FP8X4),
+                scales=y_scales[:, cols],
+                in_=rounded[h][:].rearrange("p n t -> p (n t)"),
+            )
+            nc.sync.dma_start(out=words_out[:, cols], in_=y_codes[:, cols].bitcast(I32))
+        for r in range(4):
+            queue = nc.scalar if r % 2 else nc.sync
+            queue.dma_start(
+                out=out_2[0].rearrange("(q r) n -> r q n", r=4)[r].bitcast(I32),
+                in_=y_scales[r:P:32, :].bitcast(I32),
+            )

@@ -20,10 +20,10 @@ ACT = mybir.ActivationFunctionType
 P = 128
 PASSES = 2
 CHUNKS = [
-    [(0, 1024, 1024), (1024, 1024, 384)],
-    [(0, 1024, 1024), (1024, 1024, 384)],
-    [(0, 512, 512), (512, 512, 512), (1024, 512, 512), (1536, 512, 512)],
-    [(0, 512, 512), (512, 512, 512), (1024, 512, 352), (1536, 256, 0), (1792, 256, 64)],
+    [(0, 2048, 768)],
+    [(0, 1024, 1024), (1024, 1024, 352)],
+    [(0, 1024, 1024), (1024, 1024, 640)],
+    [(0, 1024, 1024), (1024, 512, 0), (1536, 512, 160)],
 ]
 ROUND_ON_SCALAR = 192
 
@@ -66,15 +66,14 @@ def tile_moe_expert_rows_against_best_of_other_pl_kernel(
             )
 
         load_x(0, 0)
-        load_x(0, 1)
         nc.sync.dma_start(list_b[:], offs2)
         nc.sync.dma_start(list_a[:], offs)
         nc.sync.dma_start(out=of_cols[:], in_=of.rearrange("o (p c) -> (o p) c", c=4))
         for r in range(3):
             load_scales(0, r)
         load_x(1, 0)
-        load_scales(0, 3)
         load_x(1, 1)
+        load_scales(0, 3)
         for r in range(4):
             load_scales(1, r)
         for i in (2, 3):
@@ -93,8 +92,11 @@ def tile_moe_expert_rows_against_best_of_other_pl_kernel(
         spread = banks["a"][3]
         for c in range(4):
             nc.tensor.transpose(spread[:, c * P : (c + 1) * P], of_cols[:, c : c + 1].to_broadcast([P, P]), ident[:])
-        nc.vector.tensor_scalar_add(
-            of3[:].rearrange("q (p c) -> q p c", c=4), spread[:].rearrange("q (c p) -> q p c", c=4), 3.0
+        nc.scalar.activation(
+            of3[:].rearrange("q (p c) -> q p c", c=4),
+            spread[:].rearrange("q (c p) -> q p c", c=4),
+            ACT.Copy,
+            bias=3.0,
         )
 
         picked = {(e, g): keep.tile([P, 2, J], U32, name=f"picked_{e}{g}") for e in "ba" for g in range(PASSES)}

@@ -22,10 +22,10 @@ PASSES = 2
 CHUNKS = [
     [(0, 2048, 768)],
     [(0, 1024, 1024), (1024, 1024, 352)],
-    [(0, 1024, 1024), (1024, 1024, 640)],
-    [(0, 1024, 1024), (1024, 512, 0), (1536, 512, 160)],
+    [(0, 512, 512), (512, 512, 512), (1024, 1024, 416)],
+    [(0, 512, 512), (512, 512, 512), (1024, 512, 512), (1536, 512, 160)],
 ]
-ROUND_ON_SCALAR = 192
+ROUND_ON_SCALAR = 128
 
 
 def tile_moe_expert_rows_against_best_of_other_pl_kernel(
@@ -55,7 +55,7 @@ def tile_moe_expert_rows_against_best_of_other_pl_kernel(
         def load_x(i, c):
             g, u = pairs[i]
             c0, width, s_cols = CHUNKS[i][c]
-            raw[i, c] = keep.tile([P, 2, width], F32, name=f"raw{i}_{c}")
+            raw[i, c] = keep.tile([P, 2, width], F32, name=f"raw{i}_{c}", tag=f"raw{i}_{c}", align_bytes=64)
             nc.sync.dma_start(out=raw[i, c][:], in_=x_rows[g, u][:, :, c0 : c0 + width])
 
         def load_scales(w, r):
@@ -102,7 +102,7 @@ def tile_moe_expert_rows_against_best_of_other_pl_kernel(
         picked = {(e, g): keep.tile([P, 2, J], U32, name=f"picked_{e}{g}") for e in "ba" for g in range(PASSES)}
         codes, scales = {}, {}
 
-        def cast_pair(i):
+        def cast_pair(i, after_second=None):
             window = keep.tile([P, T, 2], BF16, name=f"window{i}")
             for c, (c0, width, s_cols) in enumerate(CHUNKS[i]):
                 src = raw[i, c][:].rearrange("p e c -> p c e")
@@ -110,6 +110,8 @@ def tile_moe_expert_rows_against_best_of_other_pl_kernel(
                     nc.scalar.activation(window[:, c0 : c0 + s_cols, :], src[:, 0:s_cols, :], ACT.Copy)
                 if s_cols < width:
                     nc.vector.tensor_copy(window[:, c0 + s_cols : c0 + width, :], src[:, s_cols:width, :])
+                if c == 1 and after_second:
+                    after_second()
             return window
 
         def gather(i, window, e, j0, j1):
@@ -117,13 +119,12 @@ def tile_moe_expert_rows_against_best_of_other_pl_kernel(
             words = window[:].rearrange("p c e -> p (c e)").bitcast(U32)
             nc.vector.tensor_copy(picked[e, g][:, u, j0:j1], words.indirect(lists[e][:, j0 // 16 : j1 // 16]))
 
-        woven = {
-            (e, g): keep.tile([P, 4 * J], BF16, name=f"woven_{e}{g}", align_bytes=64)
-            for e in "ba"
-            for g in range(PASSES)
-        }
+        woven = {}
 
         def weave(e, g, j0, j1, on_scalar):
+            if j0 == 0:
+                tag = "raw2_1" if (e, g) == ("a", 0) else f"woven_{e}{g}"
+                woven[e, g] = keep.tile([P, 4 * J], BF16, name=f"woven_{e}{g}", tag=tag, align_bytes=64)
             word = U32 if on_scalar else I32
             dst = woven[e, g][:].bitcast(word).rearrange("q (t p u) -> q p t u", t=4, u=2)[:, j0 // 4 : j1 // 4]
             src = picked[e, g][:, :, j0:j1].bitcast(word).rearrange("q u (p t) -> q p t u", t=4)
@@ -151,14 +152,13 @@ def tile_moe_expert_rows_against_best_of_other_pl_kernel(
                 )
 
         for i in range(3):
-            window = cast_pair(i)
+            window = cast_pair(i, (lambda: weave("a", 0, 0, J, True)) if i == 2 else None)
             for e in "ba":
                 gather(i, window, e, 0, J)
             if i == 1:
-                for e in "ba":
-                    weave(e, 0, 0, J, False)
-                for e in "ba":
-                    quantise(e, 0)
+                weave("b", 0, 0, J, False)
+                quantise("b", 0)
+        quantise("a", 0)
         window = cast_pair(3)
         for e in "ba":
             for j0 in (0, J // 2):
@@ -166,32 +166,49 @@ def tile_moe_expert_rows_against_best_of_other_pl_kernel(
                 weave(e, 1, j0, j0 + J // 2, True)
         for e in "ba":
             quantise(e, 1)
-        for g in range(PASSES):
-            for t in range(4):
-                multiply("b", g, t)
-        for t in range(4):
-            for g in range(PASSES):
-                multiply("a", g, t)
+        order = (0, 2, 1, 3)
+        for e in "ba":
+            for t in order:
+                multiply(e, 0, t)
+        multiply("b", 1, order[0])
+        for i, t in enumerate(order):
+            if i < 3:
+                multiply("b", 1, order[i + 1])
+            multiply("a", 1, t)
 
         best = keep.tile([P, 4], F32, name="best")
-        for t in range(4):
-            nc.vector.tensor_reduce(best[:, t : t + 1], banks["b"][t][:], mybir.AxisListType.X, ALU.max)
         excess = keep.tile([P, 4, N], F32, name="excess")
+        y = keep.tile([P, 4, N], F32, name="y")
         out_rows = out_0.rearrange("(p t) n -> p t n", t=4)
         half = N // 2
         rounded = [keep.tile([P, half, 4], BF16, name=f"rounded{h}", align_bytes=64) for h in range(2)]
         by_column = excess[:].rearrange("p t n -> p n t")
         split = half - ROUND_ON_SCALAR
-        for t in range(4):
-            nc.vector.scalar_tensor_tensor(
-                excess[:, t, :], banks["a"][t][:], best[:, t : t + 1], of3[:], ALU.subtract, ALU.add
-            )
-            if t == 3:
-                nc.scalar.activation(rounded[1][:, split:half, :], by_column[:, half + split : N, :], ACT.Relu)
-            y = keep.tile([P, N], F32, name=f"y{t}")
-            nc.scalar.activation(y[:], excess[:, t, :], ACT.Relu)
-            nc.sync.dma_start(out=out_rows[:, t, :], in_=y[:])
 
+        def find_best(t):
+            nc.vector.tensor_reduce(best[:, t : t + 1], banks["b"][t][:], mybir.AxisListType.X, ALU.max, negate=True)
+
+        def clip(t):
+            if False and t == order[0]:
+                shifted = keep.tile([P, N], F32, name="shifted")
+                nc.scalar.activation(shifted[:], banks["a"][t][:], ACT.Identity, bias=best[:, t : t + 1])
+                nc.gpsimd.tensor_tensor(excess[:, t, :], shifted[:], of3[:], ALU.add)
+                nc.gpsimd.tensor_scalar(y[:, t, :], excess[:, t, :], 3.0e38, 0.0, ALU.min, ALU.max)
+            else:
+                nc.vector.scalar_tensor_tensor(
+                    excess[:, t, :], banks["a"][t][:], best[:, t : t + 1], of3[:], ALU.add, ALU.add
+                )
+                nc.scalar.activation(y[:, t, :], excess[:, t, :], ACT.Relu)
+                t0 = 0 if False and t == 1 else t
+                nc.sync.dma_start(out=out_rows[:, t0 : t + 1, :], in_=y[:, t0 : t + 1, :])
+
+        find_best(order[0])
+        for i, t in enumerate(order):
+            if i < 3:
+                find_best(order[i + 1])
+            clip(t)
+
+        nc.scalar.activation(rounded[1][:, split:half, :], by_column[:, half + split : N, :], ACT.Relu)
         y_codes = keep.tile([P, N], U32, name="y_codes", align_bytes=64)
         y_scales = keep.tile([P, N], U8, name="y_scales", align_bytes=64)
         nc.vector.tensor_scalar_max(rounded[0][:], by_column[:, 0:half, :], 0.0)

from contextlib import ExitStack

import concourse.mybir as mybir
from concourse.masks import make_identity

K, T, J, N = 1024, 2048, 512, 512
FLOPS = 2 * 2 * K * J * N

F32 = mybir.dt.float32
BF16 = mybir.dt.bfloat16
I32 = mybir.dt.int32
U32 = mybir.dt.uint32
U16 = mybir.dt.uint16
U8 = mybir.dt.uint8
FP8X4 = mybir.dt.float8_e4m3fn_x4
FP4X4 = mybir.dt.float4_e2m1fn_x4
ALU = mybir.AluOpType
ACT = mybir.ActivationFunctionType

P = 128
PASSES = 2
CHUNKS = [
    [(0, 2048, 768)],
    [(0, 1024, 1024), (1024, 1024, 352)],
    [(0, 512, 512), (512, 512, 512), (1024, 1024, 416)],
    [(0, 512, 512), (512, 512, 512), (1024, 512, 512), (1536, 512, 160)],
]
ROUND_ON_SCALAR = 128


def tile_moe_expert_rows_against_best_of_other_pl_kernel(
    tc, xt, wa_words, wa_scales, wb_words, wb_scales, of, offs, offs2, out_0, out_1, out_2
):
    nc = tc.nc
    with ExitStack() as ctx:
        keep = ctx.enter_context(tc.tile_pool(name="keep", bufs=1))
        psum = ctx.enter_context(tc.psum_pool(name="psum", bufs=1))

        list_a = keep.tile([P, J // 16], U16, name="list_a")
        list_b = keep.tile([P, J // 16], U16, name="list_b")
        lists = {"a": list_a, "b": list_b}
        w_scales = keep.tile([P, 2, PASSES, N], U8, name="w_scales", align_bytes=64)
        of_cols = keep.tile([P, 4], F32, name="of_cols")
        ident = keep.tile([P, P], F32, name="ident")
        of3 = keep.tile([P, N], F32, name="of3")
        banks = {e: [psum.tile([P, N], F32, name=f"ps_{e}{t}") for t in range(4)] for e in "ba"}

        nc.vector.memset(w_scales[:].rearrange("p w g n -> p (w g n)").bitcast(I32), 0)
        make_identity(nc, ident[:])

        x_rows = xt.rearrange("(g p u e) c -> g u p e c", g=PASSES, p=P, u=2, e=2)
        pairs = [(g, u) for g in range(PASSES) for u in range(2)]
        raw = {}

        def load_x(i, c):
            g, u = pairs[i]
            c0, width, s_cols = CHUNKS[i][c]
            raw[i, c] = keep.tile([P, 2, width], F32, name=f"raw{i}_{c}", tag=f"raw{i}_{c}", align_bytes=64)
            nc.sync.dma_start(out=raw[i, c][:], in_=x_rows[g, u][:, :, c0 : c0 + width])

        def load_scales(w, r):
            src = (wb_scales, wa_scales)[w]
            nc.sync.dma_start(
                out=w_scales[r:P:32, w].bitcast(I32),
                in_=src.rearrange("g (q r) n -> r q g n", r=4)[r].bitcast(I32),
            )

        load_x(0, 0)
        nc.sync.dma_start(list_b[:], offs2)
        nc.sync.dma_start(list_a[:], offs)
        nc.sync.dma_start(out=of_cols[:], in_=of.rearrange("o (p c) -> (o p) c", c=4))
        for r in range(3):
            load_scales(0, r)
        load_x(1, 0)
        load_x(1, 1)
        load_scales(0, 3)
        for r in range(4):
            load_scales(1, r)
        for i in (2, 3):
            for c in range(len(CHUNKS[i])):
                load_x(i, c)
        w_words = {}
        for g in range(PASSES):
            wb = keep.tile([P, N], I32, name=f"wb{g}", align_bytes=64)
            nc.sync.dma_start(out=wb[:], in_=wb_words[g].rearrange("p n t -> p (n t)").bitcast(I32))
            w_words["b", g] = wb[:].bitcast(FP8X4)
        wa = keep.tile([P, PASSES, 2 * N], U8, name="wa", align_bytes=64)
        nc.sync.dma_start(out=wa[:].bitcast(I32), in_=wa_words.rearrange("g p c -> p g c").bitcast(I32))
        for g in range(PASSES):
            w_words["a", g] = wa[:, g, :].bitcast(FP4X4)

        spread = banks["a"][3]
        for c in range(4):
            nc.tensor.transpose(spread[:, c * P : (c + 1) * P], of_cols[:, c : c + 1].to_broadcast([P, P]), ident[:])
        nc.scalar.activation(
            of3[:].rearrange("q (p c) -> q p c", c=4),
            spread[:].rearrange("q (c p) -> q p c", c=4),
            ACT.Copy,
            bias=3.0,
        )

        picked = {(e, g): keep.tile([P, 2, J], U32, name=f"picked_{e}{g}") for e in "ba" for g in range(PASSES)}
        codes, scales = {}, {}

        def cast_pair(i, after_second=None):
            window = keep.tile([P, T, 2], BF16, name=f"window{i}")
            for c, (c0, width, s_cols) in enumerate(CHUNKS[i]):
                src = raw[i, c][:].rearrange("p e c -> p c e")
                if s_cols > 0:
                    nc.scalar.activation(window[:, c0 : c0 + s_cols, :], src[:, 0:s_cols, :], ACT.Copy)
                if s_cols < width:
                    nc.vector.tensor_copy(window[:, c0 + s_cols : c0 + width, :], src[:, s_cols:width, :])
                if c == 1 and after_second:
                    after_second()
            return window

        def gather(i, window, e, j0, j1):
            g, u = pairs[i]
            words = window[:].rearrange("p c e -> p (c e)").bitcast(U32)
            nc.vector.tensor_copy(picked[e, g][:, u, j0:j1], words.indirect(lists[e][:, j0 // 16 : j1 // 16]))

        woven = {}

        def weave(e, g, j0, j1, on_scalar):
            if j0 == 0:
                tag = "raw2_1" if (e, g) == ("a", 0) else f"woven_{e}{g}"
                woven[e, g] = keep.tile([P, 4 * J], BF16, name=f"woven_{e}{g}", tag=tag, align_bytes=64)
            word = U32 if on_scalar else I32
            dst = woven[e, g][:].bitcast(word).rearrange("q (t p u) -> q p t u", t=4, u=2)[:, j0 // 4 : j1 // 4]
            src = picked[e, g][:, :, j0:j1].bitcast(word).rearrange("q u (p t) -> q p t u", t=4)
            if on_scalar:
                nc.scalar.copy(dst, src)
            else:
                nc.vector.tensor_copy(dst, src)

        def quantise(e, g):
            codes[e, g] = keep.tile([P, J], U32, name=f"codes_{e}{g}", align_bytes=64)
            scales[e, g] = keep.tile([P, J], U8, name=f"scales_{e}{g}", align_bytes=64)
            nc.vector.quantize_mx(out=codes[e, g][:].bitcast(FP8X4), scales=scales[e, g][:], in_=woven[e, g][:])

        def multiply(e, g, t):
            if True:
                cols = slice(t * P, (t + 1) * P)
                nc.tensor.matmul_mx(
                    out=banks[e][t][:],
                    lhsT=codes[e, g][:, cols].bitcast(FP8X4),
                    lhsT_scale=scales[e, g][:, cols],
                    rhs=w_words[e, g],
                    rhs_scale=w_scales[:, "ba".index(e), g, :],
                    start=(g == 0),
                    stop=(g == PASSES - 1),
                )

        for i in range(3):
            window = cast_pair(i, (lambda: weave("a", 0, 0, J, True)) if i == 2 else None)
            for e in "ba":
                gather(i, window, e, 0, J)
            if i == 1:
                weave("b", 0, 0, J, False)
                quantise("b", 0)
        quantise("a", 0)
        window = cast_pair(3)
        for e in "ba":
            for j0 in (0, J // 2):
                gather(3, window, e, j0, j0 + J // 2)
                weave(e, 1, j0, j0 + J // 2, True)
        for e in "ba":
            quantise(e, 1)
        order = (0, 2, 1, 3)
        for e in "ba":
            for t in order:
                multiply(e, 0, t)
        multiply("b", 1, order[0])
        for i, t in enumerate(order):
            if i < 3:
                multiply("b", 1, order[i + 1])
            multiply("a", 1, t)

        best = keep.tile([P, 4], F32, name="best")
        excess = keep.tile([P, 4, N], F32, name="excess")
        y = keep.tile([P, 4, N], F32, name="y")
        out_rows = out_0.rearrange("(p t) n -> p t n", t=4)
        half = N // 2
        rounded = [keep.tile([P, half, 4], BF16, name=f"rounded{h}", align_bytes=64) for h in range(2)]
        by_column = excess[:].rearrange("p t n -> p n t")
        split = half - ROUND_ON_SCALAR

        def find_best(t):
            nc.vector.tensor_reduce(best[:, t : t + 1], banks["b"][t][:], mybir.AxisListType.X, ALU.max, negate=True)

        def clip(t):
            if False and t == order[0]:
                shifted = keep.tile([P, N], F32, name="shifted")
                nc.scalar.activation(shifted[:], banks["a"][t][:], ACT.Identity, bias=best[:, t : t + 1])
                nc.gpsimd.tensor_tensor(excess[:, t, :], shifted[:], of3[:], ALU.add)
                nc.gpsimd.tensor_scalar(y[:, t, :], excess[:, t, :], 3.0e38, 0.0, ALU.min, ALU.max)
            else:
                nc.vector.scalar_tensor_tensor(
                    excess[:, t, :], banks["a"][t][:], best[:, t : t + 1], of3[:], ALU.add, ALU.add
                )
                nc.scalar.activation(y[:, t, :], excess[:, t, :], ACT.Relu)
                t0 = 0 if False and t == 1 else t
                nc.sync.dma_start(out=out_rows[:, t0 : t + 1, :], in_=y[:, t0 : t + 1, :])

        find_best(order[0])
        for i, t in enumerate(order):
            if i < 3:
                find_best(order[i + 1])
            clip(t)

        nc.scalar.activation(rounded[1][:, split:half, :], by_column[:, half + split : N, :], ACT.Relu)
        y_codes = keep.tile([P, N], U32, name="y_codes", align_bytes=64)
        y_scales = keep.tile([P, N], U8, name="y_scales", align_bytes=64)
        nc.vector.tensor_scalar_max(rounded[0][:], by_column[:, 0:half, :], 0.0)
        nc.vector.tensor_scalar_max(rounded[1][:, 0:split, :], by_column[:, half : half + split, :], 0.0)
        words_out = out_1[0].rearrange("p n t -> p (n t)").bitcast(I32)
        for h in range(2):
            cols = slice(h * half, (h + 1) * half)
            nc.vector.quantize_mx(
                out=y_codes[:, cols].bitcast(FP8X4),
                scales=y_scales[:, cols],
                in_=rounded[h][:].rearrange("p n t -> p (n t)"),
            )
            nc.sync.dma_start(out=words_out[:, cols], in_=y_codes[:, cols].bitcast(I32))
        for r in range(4):
            queue = nc.scalar if r % 2 else nc.sync
            queue.dma_start(
                out=out_2[0].rearrange("(q r) n -> r q n", r=4)[r].bitcast(I32),
                in_=y_scales[r:P:32, :].bitcast(I32),
            )
